import numpy as np
import ml_dtypes


def mxq(x, axis, fmt="e4m3"):
    dtype, down = {"e4m3": (ml_dtypes.float8_e4m3fn, 7), "e5m2": (ml_dtypes.float8_e5m2, 14)}[fmt]
    v = np.moveaxis(np.asarray(x, np.float32).astype(ml_dtypes.bfloat16).astype(np.float64), axis, -1)
    blocks = v.reshape(v.shape[:-1] + (-1, 32))
    amax = np.abs(blocks).max(-1, keepdims=True)
    byte = np.maximum(np.where(amax > 0, np.frexp(amax)[1] - 1 + 127, 0) - down, 1)
    scale = np.exp2(byte - 127.0)
    codes = (blocks / scale).astype(np.float32).astype(dtype).astype(np.float64)
    return np.moveaxis((codes * scale).reshape(v.shape), -1, axis)


WIDE = False


def mx_kscale(k):
    if not WIDE:
        return np.ones(k)
    levels = np.array([10, -10, 5, -5, 0])
    if k % 512:
        return np.exp2(np.random.permutation(np.resize(levels, k // 32))).repeat(32)
    a = np.empty((k // 512, 16))
    for p in range(k // 512):
        a[p, :8] = np.random.permutation(np.resize(levels, 8))
        for g in range(8):
            far = levels[np.abs(levels - a[p, g]) >= 10]
            a[p, g + 8] = far[np.random.randint(len(far))]
    return np.exp2(a.ravel()).repeat(32)


def f64(x):
    return np.asarray(x).astype(np.float64)


def striped(idx):
    return np.tile(np.asarray(idx).reshape(-1, 16).T, (8, 1)).astype(np.uint16)


def unstriped(offs):
    return offs[:16].T.reshape(-1).astype(np.int64)


E2M1 = np.array([0.0, 0.5, 1.0, 1.5, 2.0, 3.0, 4.0, 6.0, -0.0, -0.5, -1.0, -1.5, -2.0, -3.0, -4.0, -6.0])


def pack_weight(w, fmt):
    k, n = w.shape
    w = f64(np.asarray(w, np.float32).astype(ml_dtypes.bfloat16)).reshape(k // 32, 32, n)
    amax = np.abs(w).max(1)
    if fmt == "e4m3":
        byte = np.frexp(amax)[1] - 1 + 127 - 7
    else:
        mant, ex = np.frexp(amax / 6.0)
        byte = np.where(mant > 0.5, ex, ex - 1) + 127
    byte = np.clip(np.where(amax > 0, byte, 1), 1, 254)
    scaled = (w * np.exp2(127.0 - byte)[:, None, :]).reshape(k, n).astype(np.float32)
    by_word = np.ascontiguousarray(scaled.reshape(k // 512, 128, 4, n).transpose(0, 1, 3, 2))
    if fmt == "e4m3":
        words = by_word.astype(ml_dtypes.float8_e4m3fn).view(np.uint8)
    else:
        c = by_word.astype(ml_dtypes.float4_e2m1fn).view(np.uint8) & 0xF
        words = (c[..., 0::2] | (c[..., 1::2] << 4)).reshape(k // 512, 128, 2 * n)
    return np.ascontiguousarray(words), np.ascontiguousarray(byte.astype(np.uint8).reshape(k // 512, 16, n))


def unpack_weight(words, scales, fmt):
    g, _, n = scales.shape
    words = np.ascontiguousarray(words).reshape(g, 128, n, -1)
    if fmt == "e4m3":
        vals = words.view(ml_dtypes.float8_e4m3fn).astype(np.float64)
    else:
        nib = np.empty((g, 128, n, 4), np.uint8)
        nib[..., 0::2] = words & 0xF
        nib[..., 1::2] = words >> 4
        vals = E2M1[nib]
    vals = vals * np.repeat(np.exp2(scales.astype(np.float64) - 127.0), 8, axis=1)[..., None]
    return vals.transpose(0, 1, 3, 2).reshape(g * 512, n)


B, N, T, D, DV, NQ = 1, 512, 1024, 512, 256, 256


def setup_inputs():
    n = np.random.standard_normal
    idx = np.sort(np.random.permutation(T)[:B * N].reshape(B, N), axis=1).reshape(-1)
    s = mx_kscale(D)[:, None]
    u = np.ones(T)
    u[idx] = mx_kscale(B * N)
    r = np.random.uniform(0.5, 2.0, T)
    k = n((D, T)) / s
    v = n((DV, T)) / (u * r)
    kp = pack_weight(k, "e4m3")
    when = np.zeros(T)
    when[idx] = np.sort(np.random.permutation(2 * N)[:B * N])
    return {
        "qT": (n((B, D, NQ)) * s * (1.00 / np.sqrt(D))).astype(np.float32),
        "k_words": kp[0],
        "k_scales": kp[1],
        "vT": v.astype(np.float32),
        "vs": np.tile(u * r, (128, 1)).astype(np.float32),
        "pos": np.tile(when, (128, 1)).astype(np.float32),
        "slope": np.exp2(-np.random.randint(8, 13, (B, NQ, 1))).astype(np.float32),
        "offs": striped(idx),
    }


def reference(qT, k_words, k_scales, vT, vs, pos, slope, offs):
    idx = unstriped(offs)
    k = unpack_weight(k_words, k_scales, "e4m3")
    v = f64(vT)
    pick = lambda x: x[:, idx].reshape(x.shape[0], B, N).transpose(1, 0, 2)
    q = f64(qT)
    score = mxq(q, 1, "e4m3").transpose(0, 2, 1) @ pick(k)
    score = score + f64(slope) * pick(f64(pos))[:, :1, :]
    m = score.max(-1, keepdims=True)
    p = np.exp(score - m)
    total = p.sum(-1, keepdims=True)
    w = p * pick(f64(vs))[:, :1, :]
    y = mxq(w, 2, "e4m3") @ mxq(pick(v).transpose(0, 2, 1), 1, "e4m3")
    y = y / total
    return y

from contextlib import ExitStack

import concourse.mybir as mybir
from concourse.masks import make_identity

F32 = mybir.dt.float32
BF16 = mybir.dt.bfloat16
I32 = mybir.dt.int32
U32 = mybir.dt.uint32
U16 = mybir.dt.uint16
U8 = mybir.dt.uint8
FP8X4 = mybir.dt.float8_e4m3fn_x4
ALU = mybir.AluOpType
ACT = mybir.ActivationFunctionType

P = 128
PACK = 4
NQ, N, T, D, DV = 256, 512, 1024, 512, 256
Q_TILES = NQ // P

FLOPS = 2 * NQ * N * (D + DV)


def tile_attend_alibi_srt_kernel(tc, qT, k_words, k_scales, vT, vs, pos, slope, offs, out):
    nc = tc.nc
    with ExitStack() as ctx:
        sb = ctx.enter_context(tc.tile_pool(name="sb", bufs=1))
        ps = ctx.enter_context(tc.psum_pool(name="ps", bufs=1))

        def tile(name, shape, dtype, tag=None):
            return sb.tile(shape, dtype, name=name, tag=tag or name, align_bytes=64)

        def bank(name, tag, shape):
            return ps.tile(shape, F32, name=name, tag=tag)

        offsets = sb.tile([P, N // 16], U16, name="offsets")
        key_words = tile("key_words", [P, T], U32)
        key_scales = tile("key_scales", [P, T], U8)
        pos_pool = tile("pos_pool", [P, T], F32)
        q_raw = tile("q_raw", [P, PACK, NQ], F32)
        slopes = tile("slopes", [P, Q_TILES], F32)
        ident = tile("ident", [P, P], F32)
        warm = tile("warm", [P, 1], F32, "vs_pool")
        warm_out = tile("warm_out", [P, 1], F32, "v_raw")

        nc.gpsimd.memset(key_scales[:].bitcast(I32), 0)
        nc.gpsimd.memset(warm[:], 0.0)
        nc.vector.memset(pos_pool[0:96, :], 0.0)

        nc.sync.dma_start(offsets[:], offs)
        nc.sync.dma_start(out=pos_pool[96:P, :], in_=pos[96:P, :])
        for g in range(4):
            nc.scalar.dma_start(out=key_scales[32 * g : 32 * g + 4, :].bitcast(I32), in_=k_scales[0, 4 * g : 4 * g + 4, :].bitcast(I32))
        nc.sync.dma_start(out=key_words[:].bitcast(I32), in_=k_words[0].rearrange("p t r -> p (t r)").bitcast(I32))
        nc.sync.dma_start(out=q_raw[:], in_=qT[0].rearrange("(p j) n -> p j n", j=PACK))
        nc.scalar.activation(out=warm_out[:], in_=warm[:], func=ACT.Exp)
        vs_pool = tile("vs_pool", [P, T], F32)
        nc.vector.memset(vs_pool[0:96, :], 0.0)
        nc.sync.dma_start(out=vs_pool[96:P, :], in_=vs[96:P, :])
        v_rows = vT.rearrange("(p j) t -> p j t", j=2)
        v_both = tile("v_raw", [P, 2 * T], F32)
        v_raw = [v_both[:, h * T : (h + 1) * T].rearrange("p (j t) -> p j t", j=2) for h in range(2)]
        for h in range(2):
            nc.sync.dma_start(out=v_raw[h], in_=v_rows[:, :, h * (T // 2) : (h + 1) * (T // 2)])
        make_identity(nc, ident[:])
        with nc.allow_non_contiguous_dma(reason="one slope a partition"):
            nc.gpsimd.dma_start(out=slopes[:], in_=slope[0].rearrange("(j p) o -> p (j o)", p=P))

        pos_g = tile("pos_g", [P, N], F32)
        nc.vector.tensor_copy(pos_g[:], pos_pool[:].indirect(offsets[:]))
        ks_g = tile("ks_g", [P, N], U8)
        nc.vector.tensor_copy(ks_g[:], key_scales[:].indirect(offsets[:]))
        kw_g = tile("kw_g", [P, N], U32)
        nc.vector.tensor_copy(kw_g[:], key_words[:].indirect(offsets[:]))

        def columns(name, tag, row, live):
            turned = bank(name + "_turned", tag, [P, PACK, P])
            for r in range(PACK):
                nc.tensor.transpose(turned[:, r, :], row[:, r:N:PACK], ident[:])
            cols = tile(name + "_cols", [P, PACK], F32)
            nc.scalar.copy(out=cols[:], in_=turned[:, :, live])
            return cols

        pos_cols = columns("pos", "a", pos_g, 96)
        q_bf = tile("q_bf", [P, NQ, PACK], BF16, "pos_g")
        nc.scalar.copy(out=q_bf[:], in_=q_raw[:].rearrange("p j n -> p n j"))
        q_codes = tile("q_codes", [P, NQ], U32)
        q_scales = tile("q_scales", [P, NQ], U8)
        nc.vector.quantize_mx(out=q_codes[:].bitcast(FP8X4), scales=q_scales[:], in_=q_bf[:].rearrange("p n j -> p (n j)"))

        pos_spread = bank("pos_spread", "c", [P, PACK, P])
        for r in range(PACK):
            nc.tensor.transpose(pos_spread[:, r, :], pos_cols[:, r : r + 1].to_broadcast([P, P]), ident[:])
        pos_all = tile("pos_all", [P, PACK, P], F32)
        nc.scalar.copy(out=pos_all[:], in_=pos_spread[:])

        scores = []
        for j in range(Q_TILES):
            sc = bank("scores%d" % j, "ac"[j], [P, N])
            cols = slice(j * P, (j + 1) * P)
            nc.tensor.matmul_mx(out=sc[:], lhsT=q_codes[:, cols].bitcast(FP8X4), lhsT_scale=q_scales[:, cols],
                                rhs=kw_g[:].bitcast(FP8X4), rhs_scale=ks_g[:], start=True, stop=True)
            scores.append(sc)

        vs_g = tile("vs_g", [P, N], F32, "pos_g")
        nc.vector.tensor_copy(vs_g[:], vs_pool[:].indirect(offsets[:]))

        v_pairs = tile("v_pairs", [P, T, 2], BF16, "pos_cols")
        for h in range(2):
            nc.scalar.copy(out=v_pairs[:, h * (T // 2) : (h + 1) * (T // 2), :], in_=v_raw[h].rearrange("p j t -> p t j"))

        probs, totals = [], []
        for j in range(Q_TILES):
            s = tile("s%d" % j, [P, PACK, P], F32)
            nc.vector.scalar_tensor_tensor(out=s[:], in0=pos_all[:], scalar=slopes[:, j : j + 1],
                                           in1=scores[j][:].rearrange("p (s r) -> p r s", r=PACK), op0=ALU.mult, op1=ALU.add)
            neg_max = tile("neg_max%d" % j, [P, 1], F32)
            nc.vector.tensor_reduce(out=neg_max[:], in_=s[:].rearrange("p r s -> p (r s)"), axis=mybir.AxisListType.X, op=ALU.max, negate=True)
            p = tile("p%d" % j, [P, PACK, P], F32)
            total = tile("total%d" % j, [P, 1], F32)
            nc.scalar.activation(out=p[:], in_=s[:], func=ACT.Exp, bias=neg_max[:], scale=1.0, accum_out=total[:])
            probs.append(p)
            totals.append(total)

        vs_cols = columns("vs", "a", vs_g, 96)
        v_g = tile("v_g", [P, N], U32, "pos_all")
        nc.vector.tensor_copy(v_g[:], v_pairs[:].rearrange("p t j -> p (t j)").bitcast(U32).indirect(offsets[:]))
        v_turned = bank("v_turned", "v", [P, PACK, P])
        for r in range(PACK):
            nc.tensor.transpose(v_turned[:, r, :], v_g[:].bitcast(F32)[:, r:N:PACK], ident[:])
        v_bf = tile("v_bf", [P, DV, PACK], BF16)
        nc.scalar.copy(out=v_bf[:], in_=v_turned[:].rearrange("s r w -> s (r w)").bitcast(BF16).rearrange("s (r e) -> s e r", r=PACK))
        v_codes = tile("v_codes", [P, DV], U32)
        v_scales = tile("v_scales", [P, DV], U8)

        w_q = []
        for j in range(Q_TILES):
            p_turned = bank("p_turned%d" % j, "p%d" % j, [P, PACK, P])
            for r in range(PACK):
                nc.tensor.transpose(p_turned[:, r, :], probs[j][:, r, :], ident[:])
            w_bf = tile("w_bf%d" % j, [P, P, PACK], BF16)
            nc.vector.tensor_tensor(out=w_bf[:], in0=p_turned[:].rearrange("s r q -> s q r"),
                                    in1=vs_cols[:].unsqueeze(1).to_broadcast([P, P, PACK]), op=ALU.mult)
            w_q.append(w_bf)

        inv = []
        for j in range(Q_TILES):
            r_total = tile("r_total%d" % j, [P, 1], F32)
            nc.vector.reciprocal(r_total[:], totals[j][:])
            inv.append(r_total)

        w_mx = []
        for j in range(Q_TILES):
            w_codes = tile("w_codes%d" % j, [P, P], U32)
            w_scales = tile("w_scales%d" % j, [P, P], U8)
            nc.vector.quantize_mx(out=w_codes[:].bitcast(FP8X4), scales=w_scales[:], in_=w_q[j][:].rearrange("s q r -> s (q r)"))
            w_mx.append((w_codes, w_scales))
        nc.vector.quantize_mx(out=v_codes[:].bitcast(FP8X4), scales=v_scales[:], in_=v_bf[:].rearrange("s e r -> s (e r)"))

        for j in range(Q_TILES):
            y = bank("y%d" % j, "y%d" % j, [P, DV])
            nc.tensor.matmul_mx(out=y[:], lhsT=w_mx[j][0][:].bitcast(FP8X4), lhsT_scale=w_mx[j][1][:],
                                rhs=v_codes[:].bitcast(FP8X4), rhs_scale=v_scales[:], start=True, stop=True)
            res = tile("res%d" % j, [P, DV], F32)
            nc.scalar.activation(out=res[:], in_=y[:], func=ACT.Copy, scale=inv[j][:])
            nc.sync.dma_start(out=out[0, j * P : (j + 1) * P, :], in_=res[:])
